import numpy as np, ml_dtypes
CORES = [9,25,41,57]
N = 4
import mx_ref
BF = ml_dtypes.bfloat16
def gcols(t, e):
    v = np.concatenate([t.reshape(8, 16, -1, 4), np.zeros((8, 16, 1, 4), BF)], axis=2)
    return np.ascontiguousarray(np.stack([v[g][:, e[g]] for g in range(8)])).reshape(128, -1)
def tile(rs):
    return np.stack(rs, axis=2).reshape(128, -1).astype(BF)
def pick(q, e):
    c = np.concatenate([q[0].reshape(128, -1, 4), np.zeros((128, 1, 4), np.uint8)], axis=1); s = np.concatenate([q[1], np.ones((16, 1), np.uint8)], axis=1)
    return (np.ascontiguousarray(c[:, e].reshape(128, -1)), np.ascontiguousarray(s[:, e]))
def join(*qs):
    return (np.concatenate([q[0] for q in qs], axis=1), np.concatenate([q[1] for q in qs], axis=1))
def put(q, e, v):
    c, s = q[0].reshape(128, -1, 4).copy(), q[1].copy(); c[:, e] = v[0].reshape(128, -1, 4); s[:, e] = v[1]
    return (c.reshape(128, -1), s)
def pk(c, s):
    return (np.ascontiguousarray(c), mx_ref.live(s))
def emit(q):
    return q[0], q[1]
def packed(v, rng):
    q = [mx_ref.quantize(np.ascontiguousarray(v[r])) for r in range(N)]
    return np.stack([a for a, b in q]), np.stack([mx_ref.plane(b, rng) for a, b in q])
def values_of_codes():
    e, c = np.zeros((128, 128, 4), np.float32), np.zeros((128, 2, 4), np.uint8)
    e[np.arange(128), np.arange(128), 0] = 1
    c[:127, :, 0] = np.arange(256).reshape(2, 128).T[:127]
    return mx_ref.matmul(mx_ref.quantize(e.reshape(128, 512).astype(BF)), (c.reshape(128, 8), np.full((16, 2), 127, np.uint8))).T.reshape(-1).astype(np.float64)
CODE_VALUE, SCALE_VALUE = values_of_codes(), 2.0 ** (np.arange(256) - 127.0)
def decode(q):
    return (CODE_VALUE[q[0]].reshape(16, 8, -1, 4) * SCALE_VALUE[q[1]][:, None, :, None] + 0.0).reshape(128, -1).astype(np.float32)
def f(rng, *shape):
    return mx_ref.flush((rng.standard_normal(shape, dtype=np.float32) * np.exp2(rng.integers(-2, 3, shape[:-1] + (1,)))).astype(BF))
def wide(rng, *shape, cols=0):
    v = rng.standard_normal(shape, dtype=np.float32) * np.exp2(rng.integers(-12, 13, shape)).astype(np.float32)
    if cols: v *= np.repeat(np.exp2(rng.integers(-cols, cols + 1, shape[:-2] + (1, shape[-1] // 4))) * (rng.random(shape[:-2] + (1, shape[-1] // 4)) > 0.0625), 4, axis=-1).astype(np.float32)
    return mx_ref.flush(v.astype(BF))
C, H = 384, 160
MASK = [1, 2, 3]
def big(v):
    v = v.astype(np.float32)
    v[np.abs(v) < np.float32(2.0 ** -16)] = 0
    return v.astype(BF)
def numbers_of(rng):
    return {"x": big(f(rng, N, 128, 4 * C)), "u": np.array(f(rng, N, 128, 512)), "v": np.array(f(rng, N, 128, 512))}
def layers(rng, k=1.0):
    return big(np.clip(rng.standard_normal((N, 128, 2048), dtype=np.float32), -4, 4) * np.float32(k)).reshape(N, 8, 16, 4, 8, 16, 4)
def weights(rng, w):
    c, p = packed(np.ascontiguousarray(w).reshape(N, 128, 2048), rng)
    return {"wc": c, "ws": p}
def setup_inputs(rng):
    return {**numbers_of(rng), **weights(rng, layers(rng))}
def setup_inputs_ties(rng):
    d = numbers_of(rng)
    e = rng.permutation(N)
    x = d["x"].reshape(N, 8, 16, C, 4)
    for r in range(N):
        k = rng.permutation(C) % 3
        if r == e[0]: k = np.zeros(C, int)
        elif r in e[2::2]: k = rng.permutation(3)[np.arange(C) % 3]
        a = x[r][:, :8, :3].copy()
        a[:, :, 2] = 0
        x[r][:, :8] = a[:, :, k]
    x[e[1]] = 0
    u = d["u"].reshape(N, 8, 16, 128, 4)
    for i in range(3): u[:, :, 8:, i::16] = 0
    w = layers(rng)
    w[:, :, :, :, :, :8] = 0
    return {"x": x.reshape(N, 128, 4 * C), "u": u.reshape(N, 128, 512), "v": d["v"], **weights(rng, w)}
def setup_inputs_near(rng):
    d = numbers_of(rng)
    x = d["x"].astype(np.float32).reshape(N, 8, 16, C, 4)
    x[:, :, 0] = 0
    x[:, :, 8:] = 0
    u = d["u"].reshape(N, 128, 128, 4)
    for i in range(3): u[:, :, i::16] = 0
    o = rng.permutation(N) % 4
    for r in range(N):
        k = 1.0 if o[r] == 0 else 2.0 ** -30
        if o[r] < 2:
            x[r, :, 0, :, 0] = rng.integers(0, 2, (8, C)) * 2.0 - 1.0
            s = rng.integers(0, 16, (8, C))
            x[r, :, 8] = ((s[:, :, None] >> np.arange(4)) & 1) * np.exp2(np.arange(4) - 23.0)
            x[r, :, 9, :, 0] = 2.0 ** -10
            x[r, :, 10:12, :, 0] = rng.integers(-1, 2, (8, 2, C)) * 2.0 ** -23
        else:
            x[r, :, 8, :, 0] = rng.integers(8 if o[r] == 2 else -15, 16, (8, C)) * 2.0 ** -29
            x[r, :, 10:14:2, :, 0] = rng.integers(8, 11, (8, 2, C)) * 2.0 ** -32
            x[r, :, 11:15:2, :, 0] = rng.integers(8, 10, (8, 2, C)) * 2.0 ** -32
        for g in rng.permutation(8)[:4]: x[r, g, 0 if o[r] < 2 else 8, rng.integers(C), 0] = 2.0 ** 19 * rng.choice([-1.0, 1.0])
        for h in range(0, 128, 16):
            if o[r] < 2:
                u[r, h, h, 0] = k
                u[r, h + 8, h] = k
                u[r, h + 9, h, 0] = k
                u[r, h + 10, h + 1, 0] = k
                u[r, h + 11, h + 2, 0] = k
            else:
                u[r, h + 8, h, 0] = k
                for i in range(2):
                    u[r, h + 10 + 2 * i, h + 1 + i, 0] = 1.125 * k
                    u[r, h + 11 + 2 * i, h + 1 + i, 0] = -1.25 * k
    w = layers(rng, 0.125)
    for i in [0, 8, 9, 10, 11, 12, 13, 14, 15]:
        w[:, :, i] = 0
        w[:, :, :, :, :, i] = 0
    return {"x": x.reshape(N, 128, 4 * C).astype(BF), "u": u.reshape(N, 128, 512), "v": d["v"], **weights(rng, w)}
def setup_inputs_late(rng):
    d = numbers_of(rng)
    x = d["x"].astype(np.float32).reshape(N, 8, 16, C, 4)
    k = (1 + 2 * rng.integers(0, 64, (N, 8, 8, C, 4))) * 2.0 ** -7
    a = (1.0 + k) * np.exp2(-rng.integers(8, 15, k.shape).astype(np.float64))
    a[:, :, 0, :, 0] = 1.96875
    x[:, :, 8:] = a * rng.choice([-1.0, 1.0], k.shape) * np.exp2(rng.integers(0, 3, (N, 8, 1, C, 1)).astype(np.float64))
    h = rng.permutation(8)
    x[:, h[0], 8:] *= np.float32(0.125)
    x[:, h[0], 8, :, 0] = np.where(rng.integers(0, 2, (N, C)) == 0, 3.0, 0.9375)
    x[:, h[1], 8:] = 0
    x[:, :, 0] = 0
    i = int(rng.integers(0, 2))
    for r in range(N):
        out = (r + i) % 2 == 0
        x[r, :, 0, :, 0] = 0.25 if out else -0.25
        x[r, :, 0, :, 1] = 0.25 if out or (r // 2) % 2 == 0 else -0.25
        if out:
            x[r, ::2, 0, C - 1, 0] = -0.25
            x[r, ::4, 0, C - 1, 1] = -0.25
    u = d["u"].reshape(N, 128, 128, 4)
    u[:, :, 1::16] = 0
    u[:, :, 2::16] = 0
    for g in range(0, 128, 16):
        u[:, g, g + 1, 0] = 1
        u[:, g, g + 2, 1] = 1
    w = layers(rng)
    w[:, :, :, :, h[:2], 8:] = 0
    for p in range(8, 16):
        for b in range(4):
            if p > 8 or b > 0: w[:, h[0], p, b, h[1], p, b] = 1
    return {"x": x.reshape(N, 128, 4 * C).astype(BF), "u": u.reshape(N, 128, 512), "v": d["v"], **weights(rng, w)}
def setup_inputs_ends(rng):
    d = numbers_of(rng)
    u = d["u"].reshape(N, 8, 16, 128, 4)
    for i in range(3): u[:, :, :, i::16] = 0
    x = np.zeros((N, 8, 16, C, 4))
    w = rng.choice([-1.0, 1.0], (N, 128, 2048)) * 2.0 ** -7
    most, o = 1.2890625 * 2.0 ** 29, rng.permutation(N) % 4
    for r in range(N):
        h = rng.permutation(8)
        if o[r] == 0:
            x[r] = -most * (0.9 + 0.1 * rng.random((8, 16, C, 4)))
            x[r, h[:4]] = -most
            u[r, :, :, ::32] = 2.0 ** 30
            u[r, h[:4], :, 16::32] = 2.0 ** 30
            u[r, :, :, 1::16] = -2.0 ** 30
            u[r, :, :, 2::16] = 2.0 ** 30
            w[r] = 2.0 ** -7
        if o[r] == 1:
            x[r] = most * (0.75 + 0.25 * rng.random((8, 16, C, 4))) * rng.choice([-1.0, 1.0], (8, 1, C, 1))
            for g in range(8):
                for i in (0, 1, 3): u[r, h[(g + i) % 8], :, 16 * g] = 2.0 ** 30
                if g % 2:
                    u[r, h[g - 1], :, 16 * g + 1] = 2.0 ** 30
                    u[r, h[g], :, 16 * g + 2] = -2.0 ** 30
        if o[r] == 2:
            x[r] = 2.0 ** -30
            for g in range(8):
                u[r, g, 0, 16 * g, 0] = 2.0 ** -30
                u[r, g, 0, 16 * g + 1, 0] = 2.0 ** -30 if g % 2 else -2.0 ** -30
                u[r, g, 0, 16 * g + 2, 0] = 2.0 ** -30
            w[r] = 0
        if o[r] == 3:
            x[r] = most * rng.choice([-1.0, 1.0], (8, 16, C, 4))
            for i in range(3): u[r, :, :, i::16] = (2.0 ** 30 * rng.choice([-1.0, 1.0], (8, 16, 8, 4))).astype(np.float32).astype(BF)
    d["v"] = (np.where(d["v"] < 0, -1.0, 1.0) * np.where(rng.permutation(N) % 2, 2.0 ** -30, 2.0 ** 30)[:, None, None]).astype(np.float32).astype(BF)
    return {"x": x.astype(np.float32).reshape(N, 128, 4 * C).astype(BF), "u": u.reshape(N, 128, 512), "v": d["v"], **weights(rng, w.astype(np.float32).astype(BF))}
def setup_inputs_spread(rng):
    d = numbers_of(rng)
    d["x"] = big(wide(rng, N, 128, 4 * C, cols=4))
    return {**d, **weights(rng, layers(rng, 0.125))}
def check_inputs(d):
    b = []
    for k in ("x", "u", "v"):
        a = np.abs(d[k].astype(np.float32))
        if not (np.isfinite(a).all() and ((a == 0) | (a >= 2.0 ** -30) & (a <= 2.0 ** 30)).all()): b.append("a value of " + k)
    none, least, most = [emit(mx_ref.quantize(np.full((128, 16), k, np.float32).astype(BF)))[1][0, 0] for k in (0.0, 2.0 ** -30, 2.0 ** 30)]
    n = 0.0
    for r in range(N):
        if ((d["wc"][r] == 0x7F) | (d["wc"][r] == 0xFF)).any(): b.append("wc: a code that is no number")
        s = mx_ref.live(d["ws"][r])
        if ((s != none) & ((s < least) | (s > most))).any(): b.append("ws: a scale out of range")
        n = max(n, float(np.max(np.abs(decode(pk(d["wc"][r], d["ws"][r]))))))
    m, k = float(np.max(np.abs(d["x"].astype(np.float32)))), 1.0 + 20.0 * n
    if not m * k * k * k <= 2.0 ** 30: b.append("x and W together too large")
    return b
def balls(o, out, turn):
    a, b, last = np.zeros_like(o), np.zeros_like(o), np.zeros_like(o)
    np.put_along_axis(last, o, np.zeros_like(o) + np.arange(C), axis=2)
    i, j = np.zeros((N, 8), np.int64), np.ones((N, 8), np.int64)
    n = j + 1
    for c in range(C):
        a[:, :, c] = np.take_along_axis(o, i[:, :, None], axis=2)[:, :, 0]
        b[:, :, c] = np.take_along_axis(o, j[:, :, None], axis=2)[:, :, 0]
        np.put_along_axis(last, a[:, :, c:c + 1], c, axis=2)
        i, j = np.where(out[:, :, c], n % C, np.where(turn[:, :, c], j, i)), np.where(turn[:, :, c], i, j)
        n = n + out[:, :, c]
    return a, b, last
def reference(x, u, v, wc, ws):
    qu = [mx_ref.quantize(u[r]) for r in range(N)]
    lay = [pk(wc[r], ws[r]) for r in range(N)]
    now = [x[r] for r in range(N)]
    for m in MASK:
        q = [mx_ref.quantize(now[r]) for r in range(N)]
        s = np.stack([mx_ref.matmul(qu[r], q[r]) for r in range(N)]) + np.float32(0.0)
        out = s[:, 1::16] > 0
        turn = (s[:, 2::16] > 0) & ~out
        a, b, last = balls(np.argsort(-s[:, ::16], axis=2, kind="stable"), out, turn)
        qz = []
        for r in range(N):
            t = decode(q[r]).astype(BF)
            z = (gcols(t, a[r]).astype(np.float32) + gcols(t, b[r]).astype(np.float32)) * np.float32(0.5)
            qz.append(mx_ref.quantize(z.astype(BF)))
        new = []
        for r in range(N):
            p = join(pick(qz[r ^ m], np.arange(H)), pick(qz[r], np.arange(H, C)))
            w = tile([mx_ref.matmul(pick(lay[r], np.arange(128 * k, 128 * k + 128)), p) * np.float32(0.03125) for k in range(4)])
            new.append((now[r].astype(np.float32) + gcols(w, last[r]).astype(np.float32)).astype(BF))
        now = new
    y, lb = np.zeros((N, 128, C), np.float32), np.zeros((N, 8, C), np.float32)
    oc, osc = np.zeros((N, 128, 4 * C), np.uint8), np.zeros((N, 16, C), np.uint8)
    for r in range(N):
        q = mx_ref.quantize(now[r])
        y[r] = mx_ref.matmul(mx_ref.quantize(v[r]), q)
        lb[r] = last[r]
        oc[r], osc[r] = emit(q)
    return {"y": y, "lb": lb, "oc": oc, "osc": osc}

from concourse.mybir import dt, AluOpType, ActivationFunctionType

ALU = AluOpType
ACT = ActivationFunctionType
C, H = 384, 160
R = C - H
HF = C // 2
MASKS = [1, 2, 3]
LD = "float16"
CODE = "float8_e4m3fn_x4"
EPS = 2.0 ** -110
K0 = 20
TILES = [(0, 384, (0, 21, 22, 23)), (384, 320, (17, 18, 19, 20)), (704, 256, (13, 14, 15, 16)),
         (960, 192, (9, 10, 11, 12)), (1152, 128, (5, 6, 7, 8)), (1280, 128, (1, 2, 3, 4))]
CTW = 1408


def _sb(n, d):
    return ("sbuf", [128, n], d)


SCRATCH = {
    "X": _sb(4 * C, "bfloat16"), "Xq": _sb(C, CODE), "Xs": _sb(C, "uint8"),
    "ub": _sb(512, "bfloat16"), "uq": _sb(128, CODE), "us": _sb(128, "uint8"),
    "Uq": _sb(384, CODE), "Us": _sb(384, "uint8"),
    "vb": _sb(512, "bfloat16"), "vq": _sb(128, CODE), "vs": _sb(128, "uint8"),
    "Wq": _sb(512, CODE), "Ws": _sb(512, "uint8"),
    "uof": _sb(24, "float32"), "uoff": _sb(24, "uint16"), "ioff": _sb(28, "uint16"),
    "pi": _sb(2, "int32"), "pj": _sb(2, "int32"), "pf": _sb(2, "float32"), "pc": _sb(8, "float32"),
    "jm": _sb(C, "bfloat16"), "k16": _sb(24, "float32"),
    "mask1": _sb(HF, "bfloat16"), "nmask": _sb(C, "bfloat16"), "mres": _sb(HF, "bfloat16"),
    "t16": _sb(48, "bfloat16"), "madd": _sb(448, "bfloat16"), "Tq": _sb(4 * C, "bfloat16"),
    "Zq0": _sb(H, CODE), "Zs0": _sb(H, "uint8"),
    "ones": _sb(516, "bfloat16"), "eb": _sb(516, "bfloat16"), "Eq": _sb(512, CODE), "Es": _sb(512, "uint8"),
    "G": _sb(128, "bfloat16"), "WB": _sb(1024, "bfloat16"), "Gq": _sb(256, CODE), "Gs": _sb(256, "uint8"),
    "cval": _sb(400, "bfloat16"), "c1": _sb(24, "float32"), "cwm": _sb(24, "float32"), "cst": _sb(24, "float32"),
    "eps": _sb(2, "float32"),
    "CT": _sb(4 * CTW, "bfloat16"), "Cq": _sb(CTW, CODE), "Cs": _sb(CTW, "uint8"),
    "Ym": _sb(C, "float32"), "Ys": _sb(C, "float32"),
    "o2": _sb(C, "bfloat16"), "tt": _sb(C, "bfloat16"), "outs": _sb(C, "bfloat16"), "Bm": _sb(C, LD),
    "rr": _sb(C + 2, "bfloat16"), "Am": _sb(C, "bfloat16"), "K": _sb(C, LD),
    "P": _sb(C + 2, LD), "dl": _sb(C + 2, LD), "EX": _sb(2 * C, LD), "PW": _sb(72, "float32"),
    "pl": _sb(48, "uint16"), "s1": _sb(24, "float32"),
    "Rs": _sb(24, "float32"), "RW": _sb((24 - K0) * C, LD), "RD": _sb(C, LD), "RL": _sb(C, LD), "Rb": _sb(24, "float32"), "Rc": _sb(24, "float32"),
    "Ec": _sb(C, "float32"), "sw": _sb(24, "float32"), "su": _sb(24, "uint16"),
    "ow": _sb(C + 16, "bfloat16"), "AB": _sb(2 * C, "bfloat16"), "EZ": _sb(2 * C, LD), "zl": _sb(48, "uint16"),
    "Tp": _sb(4 * C, "bfloat16"), "Ta": _sb(4 * C, "bfloat16"), "Z": _sb(4 * C, "bfloat16"),
    "Zq": _sb(R, CODE), "Zs": _sb(R, "uint8"), "Vp": _sb(4 * C, "bfloat16"),
    "A2": _sb(C, "bfloat16"), "B2": _sb(C, "bfloat16"), "K2": _sb(C, "bfloat16"), "sc": _sb(C, LD), "scf": _sb(2, "float32"),
    "Kx": _sb(C, LD),
    "sm": _sb(24 * 10, "float32"), "lo": _sb(24, "uint16"), "Lw": _sb(800, "bfloat16"),
    "lv": _sb(C, "bfloat16"), "El": _sb(C, LD), "ll": _sb(24, "uint16"), "lf": _sb(C, "float32"),
    "yb": _sb(C, "float32"),
}
for _r in range(3):
    SCRATCH["lc%d" % _r] = _sb(C, CODE)
    SCRATCH["ls%d" % _r] = _sb(C, "uint8")
    SCRATCH["lz%d" % _r] = _sb(20, "uint16")
for _b in range(8):
    SCRATCH["P%d" % _b] = ("psum", [128, 512], "float32")

SEMAPHORES = ["qV", "qA", "qT", "qG", "dx0", "dx1", "du", "dv", "dw", "dout", "sentx", "sentl",
              "arx0", "arx1", "arx2", "arl0", "arl1", "arl2"]


def rank_program(g, core, T, topo):
    rank = T.rank_of(core)
    if rank is None:
        return
    Q = {"V": g.vector, "A": g.scalar, "T": g.tensor, "G": g, "S": g.sync}
    known = {e: {} for e in Q}
    total = {}
    lastw, readers = {}, {}
    pend = {e: [] for e in Q}

    def need(e, evs):
        best = {}
        for ev in evs:
            if ev[0] not in best or best[ev[0]][1] < ev[1]:
                best[ev[0]] = ev
        for ev in sorted(best.values(), key=lambda v: -len(v[2])):
            if known[e].get(ev[0], 0) < ev[1]:
                Q[e].wait_ge(T.sem[ev[0]], ev[1])
                known[e][ev[0]] = ev[1]
                for s, n in ev[2].items():
                    if known[e].get(s, 0) < n:
                        known[e][s] = n

    def emit(e, fn, rd, wr, sem, inc):
        rd = [k.split("@")[0] for k in rd]
        wr = [k.split("@")[0] for k in wr]
        own = "q" + e if sem is None else None
        evs = []
        for k in rd:
            if k in lastw:
                evs.append(lastw[k])
            if k[0] == "P" and k[1:].isdigit():
                evs += [v for v in readers.get(k, []) if v[0] != own]
        for k in wr:
            if k in lastw and lastw[k][0] != own:
                evs.append(lastw[k])
            evs += [v for v in readers.get(k, []) if v[0] != own]
        need(e, evs)
        s = sem or own
        ins = fn()
        if ins is not None:
            ins.then_inc(T.sem[s], inc)
        total[s] = total.get(s, 0) + inc
        ev = (s, total[s], dict(known[e]))
        for k in rd:
            readers.setdefault(k, []).append(ev)
        for k in wr:
            lastw[k] = ev
            readers[k] = []

    def op(e, fn, rd, wr, sem=None, inc=1):
        pend[e].append((e, fn, rd, wr, sem, inc))

    def flush():
        left = {}
        for e in pend:
            for o in pend[e]:
                for k in o[3]:
                    left[k] = left.get(k, 0) + 1
        while any(pend.values()):
            moved = False
            for e in pend:
                while pend[e] and all(left.get(k, 0) - (k in pend[e][0][3]) == 0 for k in pend[e][0][2]):
                    o = pend[e].pop(0)
                    emit(*o)
                    for k in o[3]:
                        left[k] -= 1
                    moved = True
            assert moved, [(e, pend[e][0][2:4]) for e in pend if pend[e]]

    v, a, pe = g.vector, g.scalar, g.tensor

    def ts(out, in0, s1, s2, o0, o1, rd, wr):
        if o1 is None:
            op("V", lambda: v.tensor_scalar(out, in0, s1, None, o0), rd, wr)
        else:
            op("V", lambda: v.tensor_scalar(out, in0, s1, s2, o0, o1), rd, wr)

    def tt(out, in0, in1, o, rd, wr):
        op("V", lambda: v.tensor_tensor(out, in0, in1, o), rd, wr)

    def scan(out, d0, d1, init, o0, o1, rd, wr):
        op("V", lambda: v.tensor_tensor_scan(out, d0, d1, init, o0, o1), rd, wr)

    def cp(out, in_, rd, wr):
        op("V", lambda: v.tensor_copy(out, in_), rd, wr)

    def ms(ap, c, wr):
        op("V", lambda: v.memset(ap, c), [], wr)

    def qz(c, s, t, rd, wr):
        op("V", lambda: v.quantize_mx(c, s, t), rd, wr)

    def act(out, in_, f, rd, wr, **kw):
        op("A", lambda: a.activation(out, in_, f, **kw), rd, wr)

    def mm(bank, n, lq, ls, rq, rs, rd, start=True, stop=True):
        op("T", lambda: pe.matmul_mx(T[bank.split("@")[0]][:, 0:n], lq, ls, rq, rs, start, stop), rd, [bank])

    def iota(out, pat, base, cm, wr, flag=True):
        if flag:
            op("G", lambda: g.iota(out, pat, base, cm, allow_small_or_imprecise_dtypes=True), [], wr)
        else:
            op("G", lambda: g.iota(out, pat, base, cm), [], wr)

    def sel(out, in_, pat, cmp, base, cm, rd, wr):
        op("G", lambda: g.affine_select(out, in_, pat, cmp, 0.0, base, cm), rd, wr)

    def dma(e, out, in_, sem, rd, wr):
        op(e, lambda: Q[e].dma_start(out, in_), rd, wr, sem=sem, inc=16)

    def xk(h):
        return ["X%d%d" % (h, b) for b in range(4)]

    slot = {}
    for (c0, n, ks) in TILES:
        for t, k in enumerate(ks):
            slot[k] = (4 * c0 + t, C if k == 0 else 16 * k)

    def sl(k, lo=0, hi=None):
        o, w = slot[k]
        return T.CT[:, o + 4 * lo:o + 4 * (w if hi is None else hi) - 3:4]

    def small(i):
        return T.sm[:, 24 * i:24 * i + 24]

    dma("A", T.ub[:], T.u[:], "du", [], ["ub"])
    dma("S", T.X[:, 0:4 * HF], T.x[:, 0:4 * HF], "dx0", [], xk(0))
    dma("S", T.X[:, 4 * HF:4 * C], T.x[:, 4 * HF:4 * C], "dx1", [], xk(1))
    dma("S", T.Wq[:].bitcast(dt.uint8), T.wc[:], "dw", [], ["W"])
    dma("S", T.Ws[:], T.ws[:], "dw", [], ["W"])
    dma("S", T.vb[:], T.v[:], "dv", [], ["vb"])

    iota(T.pi[:], [[1, 2]], 0, 1, ["pi"], flag=False)
    iota(T.uof[:], [[1, 3], [16, 8]], 0, 0, ["uof"])
    iota(T.jm[:], [[0, 24], [1, 16]], 0, 0, ["jm"])
    iota(T.k16[:], [[16, 24]], 0, 0, ["k16"])
    sel(T.eb[:], T.ones[:], [[1, 516]], ALU.is_equal, -3, -4, ["ones"], ["eb"])
    sel(T.G[:], T.ones[:, 0:128], [[-16, 8], [0, 16]], ALU.is_ge, 0, 1, ["ones"], ["G@0"])
    sel(T.G[:], T.G[:], [[16, 8], [0, 16]], ALU.is_ge, 15, -1, ["G@0"], ["G"])
    sel(T.WB[:, 0:512:4], T.G[:], [[1, 128]], ALU.is_gt, 0, -1, ["G"], ["WB0"])
    iota(T.cval[:], [[1, 400]], -192, 0, ["cval@0"])
    ms(T.ones[:], 1.0, ["ones"])
    ms(T.eps[:, 0:1], EPS, ["eps"])
    ms(T.eps[:, 1:2], -EPS, ["eps"])
    ts(T.pj[:], T.pi[:], 15, None, ALU.bitwise_and, None, ["pi"], ["pj"])
    cp(T.uoff[:], T.uof[:], ["uof"], ["uoff"])
    ms(T.rr[:, 0:1], -1.0, ["rr0"])
    cp(T.pf[:], T.pj[:], ["pj"], ["pf"])
    ms(T.P[:, 0:1], -1.0, ["rr0"])
    ms(T.dl[:, 0:1], -1.0, ["rr0"])
    ms(T.Rs[:, 0:1], 0.0, ["rr0"])
    ts(T.pc[:, 0:1], T.pf[:, 0:1], 15.0, -1024.0, ALU.is_lt, ALU.mult, ["pf"], ["pc0"])
    ts(T.pc[:, 3:4], T.pf[:, 0:1], -1.0, 16.0, ALU.mult, ALU.add, ["pf"], ["pc3"])
    ts(T.pc[:, 1:2], T.pc[:, 0:1], 192.0, None, ALU.add, None, ["pc0"], ["pc1"])
    ts(T.pc[:, 2:3], T.pc[:, 0:1], 1.0, None, ALU.add, None, ["pc0"], ["pc2"])
    ts(T.pc[:, 4:5], T.pc[:, 0:1], -1.0, -601.0, ALU.mult, ALU.add, ["pc0"], ["pc4"])
    ts(T.t16[:, 16:32], T.jm[:, 0:16], T.pf[:, 0:1], -4096.0, ALU.is_equal, ALU.mult, ["jm", "pf"], ["ta"])
    ts(T.t16[:, 32:48], T.jm[:, 0:16], T.pf[:, 1:2], 1024.0, ALU.is_equal, ALU.mult, ["jm", "pf"], ["tb"])
    ts(T.ioff[:], T.jm[:, 0:28], 0.0, T.pf[:, 0:1], ALU.mult, ALU.add, ["jm", "pf"], ["ioff"])
    ts(T.mask1[:], T.jm[:, 0:HF], T.pf[:, 0:1], None, ALU.is_equal, None, ["jm", "pf"], ["mask1"])
    tt(T.t16[:, 0:16], T.t16[:, 16:32], T.t16[:, 32:48], ALU.add, ["ta", "tb"], ["t0"])
    ts(T.mres[:], T.jm[:, 0:HF], 0.0, None, ALU.is_gt, None, ["jm"], ["mres"])
    ts(T.nmask[:], T.jm[:], T.pf[:, 0:1], None, ALU.not_equal, None, ["jm", "pf"], ["nmask"])
    ts(T.c1[:], T.k16[:], T.pc[:, 0:1], T.pc[:, 3:4], ALU.add, ALU.add, ["k16", "pc0", "pc3"], ["kc1"])
    ts(T.cwm[:], T.k16[:], T.pf[:, 0:1], -383.0, ALU.add, ALU.add, ["k16", "pf"], ["cwm"])
    ts(T.s1[:], T.cwm[:], 0.0, None, ALU.not_equal, None, ["cwm"], ["s1"])
    ts(T.cst[:], T.cwm[:], 768.0, None, ALU.add, None, ["cwm"], ["cst@0"])
    tt(T.cst[:], T.cst[:], T.s1[:], ALU.mult, ["cst@0", "s1"], ["cst"])
    qz(T.uq[:], T.us[:], T.ub[:], ["ub"], ["uq"])
    cp(T.Uq[:, 0:128].bitcast(dt.uint32), T.uq[:].bitcast(dt.uint32).indirect(T.uoff[:, 0:8]), ["uq", "uoff"], ["Uq0"])
    for (c0, n, ks) in TILES:
        w = n - 16 * min(k for k in ks if k)
        act(T.CT[:, 4 * (c0 + n - w):4 * (c0 + n)], T.ones[:, 0:4 * w], ACT.Copy, ["ones"], ["pad"], scale=0.0)
    act(T.madd[:], T.t16[:, 0:16].indirect(T.ioff[:]), ACT.Copy, ["t0", "ioff"], ["madd"])
    act(T.Us[:, 0:128], T.us[:].indirect(T.uoff[:, 0:8]), ACT.Copy, ["uq", "uoff"], ["Us0"])
    act(T.Us[:, 128:384], T.us[:].indirect(T.uoff[:, 8:24]), ACT.Copy, ["uq", "uoff"], ["Us1"])
    for t in (1, 2, 3):
        act(T.WB[:, t:512:4], T.G[:], ACT.Copy, ["G"], ["WB%d" % t])
    for t in range(4):
        act(T.WB[:, 512 + t:1024:4], T.G[:], ACT.Copy, ["G"], ["WB%d" % (4 + t)])

    def xstep(h, b):
        xs = T.X[:, 4 * HF * h + b:4 * HF * (h + 1):4]
        tt(xs, T.Vp[:, C * b:C * b + C].indirect(T.ll[:, 12 * h:12 * h + 12]), xs, ALU.add,
           ["Va%d@" % b, "Vb%d@" % b, "ll@", "X%d%d" % (h, b)], ["X%d%d" % (h, b)])

    def qx(h):
        qz(T.Xq[:, HF * h:HF * h + HF], T.Xs[:, HF * h:HF * h + HF], T.X[:, 4 * HF * h:4 * HF * (h + 1)], xk(h), ["Xq%d" % h])

    def ym(h, bank):
        tt(T.Ym[:, HF * h:HF * h + HF], T[bank[:2]][:, HF * h:HF * h + HF], T.mask1[:, 0:HF], ALU.mult, [bank, "mask1"], ["Ym%d" % h])

    def ysc(h):
        scan(T.Ys[:, HF * h:HF * h + HF], T.mres[:, 0:HF], T.Ym[:, HF * h:HF * h + HF], 0.0, ALU.mult, ALU.add,
             ["mres", "Ym%d" % h], ["Ys%d" % h])

    def ge(h, bank):
        tt(sl(0, HF * h, HF * h + HF), T[bank[:2]][:, HF * h:HF * h + HF], T.Ys[:, HF * h:HF * h + HF], ALU.is_le,
           [bank, "Ys%d" % h, "pad"], ["c0"])

    for rnd in range(3):
        first, last = rnd == 0, rnd == 2
        mate = T.cores[rank ^ MASKS[rnd]]
        lc, ls, lz = T["lc%d" % rnd], T["ls%d" % rnd], T["lz%d" % rnd]
        lastw["landx%d" % rnd] = ("arx%d" % rnd, 2 * len(topo.engines(mate, core)), {})
        lastw["landl%d" % rnd] = ("arl%d" % rnd, len(topo.engines(mate, core)), {})
        XQ = ["Xq0", "Xq1"]
        rid, pid, _se = topo.addr(mate)

        def send(o, i, arr, sent, rd, pid=pid, rid=rid, mate=mate):
            def call():
                g.remote_dma(o, i, T.sem[arr], T.sem[sent], pid, rid, topo.mask(core, mate))
            op("G", call, rd, [], sem=sent, inc=len(topo.engines(core, mate)))

        send(lc[:].bitcast(dt.uint8), T.Xq[:].bitcast(dt.uint8), "arx%d" % rnd, "sentx", XQ)
        send(ls[:], T.Xs[:], "arx%d" % rnd, "sentx", XQ)

        def umm(bank, i, n):
            mm(bank, n, T.Uq[:, 128 * i:128 * i + 128], T.Us[:, 128 * i:128 * i + 128], T.Xq[:, 0:n], T.Xs[:, 0:n],
               ["Uq%d" % min(i, 1), "Us%d" % min(i, 1)] + XQ[:n // HF])

        def ys(k):
            return T.Ys[:, 16 * k + 15:16 * k + 16]

        def vpass(k):
            if k >= K0:
                ts(sl(k), T.P4[:, 0:16 * k], ys(k), None, ALU.is_lt, None, ["P4@s", "Ys1", "pad"], ["c%d" % k])

        def vrow(k):
            if k >= K0:
                j = k - K0
                scan(T.RW[:, C * (j + 1) - 16 * k:C * (j + 1)], sl(k), sl(k), 0.0, ALU.add, ALU.max, ["c%d" % k], ["RW%d" % k])

        def lpass(k):
            ts(sl(k), T.P1[:, 0:16 * k], ys(k), None, ALU.is_lt, None, ["P1@s", "Ys0", "pad"], ["c%d" % k])

        def lrow(k):
            e = HF * (k - 9)
            scan(T.RL[:, e - 16 * k:e], sl(k), sl(k), 0.0, ALU.add, ALU.max, ["c%d" % k], ["RL%d" % k])

        def a1(k):
            bank = "P0@s" if k < 12 else "P5@s"
            act(sl(k), T[bank[:2]][:, 0:16 * k], ACT.Sign, [bank, "Ys%d" % (k // 12), "pad"], ["c%d@1" % k], bias=ys(k), scale=-1.0)

        def a2(k):
            act(sl(k), sl(k), ACT.Relu, ["c%d@1" % k], ["c%d" % k, "R%d" % k], accum_out=T.Rs[:, k:k + 1])

        def arun(ks):
            for i, k in enumerate(ks):
                a1(k)
                if i:
                    a2(ks[i - 1])
            a2(ks[-1])

        def quant(ti, stop=False):
            c0, n, ks = TILES[ti]
            qz(T.Cq[:, c0:c0 + n], T.Cs[:, c0:c0 + n], T.CT[:, 4 * c0:4 * (c0 + n)], ["c%d" % k for k in ks] + ["pad"], ["Cq%d" % ti])

        def cmm(ti, stop=False):
            c0, n, ks = TILES[ti]
            w0 = 0 if ti == 0 else 128
            mm("P6@c", n, T.Gq[:, w0:w0 + 128], T.Gs[:, w0:w0 + 128], T.Cq[:, c0:c0 + n], T.Cs[:, c0:c0 + n],
               ["Gq", "Cq%d" % ti], start=ti == 0, stop=stop)

        TB = ["P7@t", "P1@t", "P2@t", "P3@t"]

        umm("P1@s", 0, HF)
        umm("P0@s", 0, HF)
        umm("P4@s", 0, C)
        umm("P2@s", 1, C)
        umm("P3@s", 2, C)
        umm("P5@s", 0, C)
        cmm(0)
        for b in range(4):
            mm(TB[b], C, T.Eq[:, 128 * b:128 * b + 128], T.Es[:, 128 * b:128 * b + 128], T.Xq[:], T.Xs[:],
               ["Eq", "c0", "c10", "o2", "tt"] + XQ)
        cmm(4)
        cmm(3)
        cmm(1)
        cmm(2)
        cmm(5, True)
        TM = ["P0@m", "P4@m", "P5@m", "P7@m"]
        for b in range(4):
            mm(TM[b], C, T.Eq[:, 128 * b:128 * b + 128], T.Es[:, 128 * b:128 * b + 128], lc[:], ls[:],
               ["Eq", "landx%d" % rnd, "Tp0"])

        if not first:
            act(T.Lw[:, 0:C + 1], T.cval[:, 0:C + 1], ACT.Copy, ["cval", "cval@0"], ["Lw@0"])
        arun([9, 8, 7, 6, 5])
        act(T.tt[:], T.P3[:, 0:C], ACT.Sign, ["P3@s", "eps"], ["tt"], bias=T.eps[:, 0:1], scale=-1.0)
        act(T.o2[:], T.P2[:, 0:C], ACT.Sign, ["P2@s", "eps"], ["o2"], bias=T.eps[:, 1:2])
        arun([12] + list(range(K0 - 1, 12, -1)) + [4, 3, 2, 1])
        act(T.A2[:], T.tt[:], ACT.Copy, ["tt"], ["A2"], scale=0.5 - 2.0 ** -10, bias=0.5 + 2.0 ** -10)
        act(T.B2[:], T.o2[:], ACT.Copy, ["o2"], ["B2"], scale=2.0 ** 18 - 2.0 ** 8, bias=2.0 ** 18 + 2.0 ** 8)
        for b in range(4):
            act(T.Tp[:, C * b:C * b + C], T[TB[b][:2]][:, 0:C], ACT.Copy, [TB[b]], ["Tp%d" % b], scale=0.5)
        if first:
            act(T.Lw[:, 0:C + 1], T.cval[:, 0:C + 1], ACT.Copy, ["cval", "cval@0"], ["Lw@0"])

        def unpack(b):
            act(T.Tq[:, C * b:C * b + C], T[TM[b][:2]][:, 0:C], ACT.Copy, [TM[b]], ["Tq%d" % b], scale=0.5)

        unpack(0)
        unpack(1)
        unpack(2)

        if first:
            def qe(b):
                qz(T.Eq[:, 128 * b:128 * b + 128], T.Es[:, 128 * b:128 * b + 128], T.eb[:, 3 - b:515 - b], ["eb"], ["Eq"])
            qx(0)
            cp(T.Uq[:, 128:384].bitcast(dt.uint32), T.uq[:].bitcast(dt.uint32).indirect(T.uoff[:, 8:24]), ["uq", "uoff"], ["Uq1"])
            ym(0, "P1@s")
            qe(0)
            ysc(0)
            qx(1)
            qe(1)
            qe(2)
            qe(3)
        else:
            for b in range(4):
                xstep(0, b)
            xstep(1, 0)
            qx(0)
            xstep(1, 1)
            ym(0, "P1@s")
            xstep(1, 2)
            ysc(0)
            xstep(1, 3)
            qx(1)
        ge(0, "P1@s")
        lpass(11)
        ym(1, "P4@s")
        if first:
            ms(T.cval[:, C:C + 1], -256.0, ["cval"])
        lpass(10)
        ysc(1)
        lrow(11)
        if first:
            qz(T.Gq[:], T.Gs[:], T.WB[:], ["WB%d" % t for t in range(8)], ["Gq"])
        ge(1, "P4@s")
        lrow(10)
        vpass(23)
        cp(T.Rs[:, 10:12], T.RL[:, HF - 1:C:HF], ["RL10", "RL11"], ["R10", "R11"])
        vpass(22)
        vpass(21)
        scan(T.RD[:], T.nmask[:], sl(0), 0.0, ALU.mult, ALU.add, ["nmask", "c0"], ["RD"])
        quant(0)
        scan(T.rr[:, 1:C + 1], T.tt[:], T.o2[:], -1.0, ALU.mult, ALU.max, ["tt", "o2"], ["rr"])
        ts(T.Bm[:], T.o2[:], -200.0, 801.0, ALU.mult, ALU.add, ["o2"], ["Bm"])
        ts(T.Am[:], T.rr[:, 0:C], -300.0, 300.0, ALU.mult, ALU.add, ["rr", "rr0"], ["Am"])
        ts(T.outs[:], T.o2[:], -0.5, -0.5, ALU.mult, ALU.add, ["o2"], ["outs"])
        scan(T.K[:], T.Am[:], T.Bm[:], -1.0, ALU.max, ALU.subtract, ["Am", "Bm"], ["K"])
        quant(4)
        vpass(20)
        scan(T.P[:, 1:C + 1], T.outs[:], T.outs[:], -1.0, ALU.add, ALU.min, ["outs"], ["P"])
        scan(T.dl[:, 1:C + 1], T.outs[:], T.K[:], -1.0, ALU.add, ALU.max, ["outs", "K"], ["dl"])
        quant(3)
        vpass(19)
        vpass(18)
        vpass(17)
        scan(T.EX[:, C:2 * C], T.madd[:, 0:C], T.P[:, 0:C], 0.0, ALU.add, ALU.max, ["madd", "P", "rr0"], ["EXa"])
        scan(T.EX[:, 0:C], T.madd[:, 0:C], T.dl[:, 0:C], 0.0, ALU.add, ALU.max, ["madd", "dl", "rr0"], ["EXb"])
        tt(T.Rb[:], T.c1[:], T.RD[:, 15:C:16], ALU.subtract, ["kc1", "RD"], ["Rb"])
        vrow(23)
        ts(T.PW[:, 0:48], T.EX[:, 15:2 * C:16], T.pc[:, 0:1], -1.0, ALU.add, ALU.mult, ["EXa", "EXb", "pc0"], ["PW"])
        vrow(22)
        quant(1)
        tt(T.PW[:, 48:72], T.PW[:, 24:48], T.PW[:, 0:24], ALU.subtract, ["PW"], ["PB"])
        vrow(21)
        vrow(20)
        vrow(19)
        vrow(18)
        vrow(17)
        cp(T.pl[:], T.PW[:, 24:72], ["PW", "PB"], ["pl"])
        quant(2)
        tt(T.Rc[:, K0:24], T.Rb[:, K0:24], T.RW[:, C - 1:(24 - K0) * C:C], ALU.subtract,
           ["Rb"] + ["RW%d" % k for k in range(K0, 24)], ["Rca"])
        quant(5)
        tt(T.Rc[:, 0:K0], T.Rb[:, 0:K0], T.Rs[:, 0:K0], ALU.subtract, ["Rb", "rr0"] + ["R%d" % k for k in range(1, K0)], ["Rcb"])
        kx = T.Kx[:, 15:C:16]
        scan(T.Kx[:], T.madd[:, 0:C], T.K[:], 0.0, ALU.add, ALU.max, ["madd", "K"], ["Kx"])
        scan(T.Ec[:], T.madd[:, 0:C], T.P6[:, 0:C], 0.0, ALU.add, ALU.max, ["madd", "P6@c"], ["Ec"])
        ts(small(0), kx, T.pc[:, 4:5], 600.0, ALU.is_le, ALU.mult, ["Kx", "pc4"], ["m0"])
        tt(T.sw[:], T.Ec[:, 15:C:16], T.Rc[:], ALU.add, ["Ec", "Rca", "Rcb"], ["sw"])
        tt(small(1), small(0), kx, ALU.add, ["Kx", "m0"], ["m1"])
        cp(T.su[:], T.sw[:], ["sw"], ["su"])
        tt(small(6), small(0), T.PW[:, 0:24], ALU.min, ["m0", "PW"], ["m6"])
        cp(T.ow[:, 0:C].indirect(T.su[:]), T.cval[:, 0:C], ["su", "cval", "cval@0"], ["ow"])
        scan(T.K2[:], T.A2[:], T.B2[:], 1.0, ALU.min, ALU.mult, ["A2", "B2"], ["K2"])
        act(T.ow[:, C:C + 1], T.ow[:, 0:1], ACT.Copy, ["ow"], ["owx"])
        act(T.AB[:, 0:H], T.ow[:, 0:C].indirect(T.pl[:, 0:10]), ACT.Copy, ["ow", "pl"], ["AB0"])
        act(T.AB[:, 2 * H + R:2 * C], T.ow[:, 0:C].indirect(T.pl[:, 34:48]), ACT.Copy, ["ow", "pl"], ["AB3"])
        act(T.AB[:, 2 * H:2 * H + R], T.ow[:, 0:C + 1].indirect(T.pl[:, 10:24]), ACT.Copy, ["ow", "owx", "pl"], ["AB2"])
        unpack(3)
        cp(T.AB[:, H:2 * H], T.ow[:, 0:C].indirect(T.pl[:, 24:34]), ["ow", "pl"], ["AB1"])
        scan(T.sc[:, 0:C - 1], T.ones[:, 0:C - 1], T.K2[:, 0:C - 1], 1.0, ALU.add, ALU.min, ["K2", "ones"], ["sc"])
        scan(T.EZ[:, 0:2 * H], T.madd[:, 0:2 * H], T.AB[:, 0:2 * H], 0.0, ALU.add, ALU.max, ["madd", "AB0", "AB1"], ["EZ0"])
        ts(small(2), small(1), T.pc[:, 2:3], -2.0, ALU.add, ALU.mult, ["m1", "pc2"], ["m2"])
        ts(T.zl[:, 0:20], T.EZ[:, 15:2 * H:16], T.pc[:, 1:2], None, ALU.add, None, ["EZ0", "pc1"], ["zl0"])
        send(lz[:], T.zl[:, 0:20], "arl%d" % rnd, "sentl", ["zl0"])

        def means(c0, n, src, nm, la, key):
            for b in range(4):
                act(T.Ta[:, C * b + c0:C * b + c0 + n], src[:, C * b:C * b + C].indirect(la), ACT.Copy,
                    ["%s%d" % (nm, b), key], ["Ta%d%d" % (b, c0)])

        def mean(b, c0, n, src, nm, lb, key):
            tt(T.Z[:, 4 * c0 + b:4 * (c0 + n):4], src[:, C * b:C * b + C].indirect(lb), T.Ta[:, C * b + c0:C * b + c0 + n],
               ALU.add, ["%s%d" % (nm, b), key, "Ta%d%d" % (b, c0)], ["Z%d%d" % (b, c0)])

        cp(T.scf[:, 0:1], T.sc[:, C - 2:C - 1], ["sc"], ["scf"])
        tt(small(5), small(2), T.cst[:], ALU.min, ["m2", "cst"], ["m5"])
        ts(small(4), T.cwm[:], T.scf[:, 0:1], 0.0, ALU.add, ALU.not_equal, ["cwm", "scf"], ["m4"])
        tt(small(8), small(6), T.PW[:, 48:72], ALU.add, ["m6", "PB"], ["m8"])
        tt(small(7), small(5), small(4), ALU.mult, ["m5", "m4"], ["m7"])
        scan(T.EZ[:, 2 * H:2 * C], T.madd[:, 0:2 * R], T.AB[:, 2 * H:2 * C], 0.0, ALU.add, ALU.max, ["madd", "AB2", "AB3"], ["EZ1"])
        tt(small(9), small(8), small(7), ALU.max, ["m8", "m7"], ["m9"])
        ts(T.zl[:, 20:48], T.EZ[:, 2 * H + 15:2 * C:16], T.pc[:, 1:2], None, ALU.add, None, ["EZ1", "pc1"], ["zl1"])
        cp(T.lo[:], small(9), ["m9"], ["lo"])
        if first:
            qz(T.vq[:], T.vs[:], T.vb[:], ["vb"], ["vq"])
        cp(T.Lw[:].indirect(T.lo[:]), T.cval[:, 0:C], ["lo", "cval", "Lw@0"], ["Lw@1"])
        mean(0, H, R, T.Tp, "Tp", T.zl[:, 34:48], "zl1")
        ts(T.Lw[:, 0:1], T.Lw[:, 0:1], T.Lw[:, C:C + 1], None, ALU.max, None, ["Lw@1"], ["Lw"])
        for b in range(1, 4):
            mean(b, H, R, T.Tp, "Tp", T.zl[:, 34:48], "zl1")
        mean(0, 0, H, T.Tq, "Tq", lz[:, 10:20], "landl%d" % rnd)
        qz(T.Zq[:], T.Zs[:], T.Z[:, 4 * H:4 * C], ["Z%d%d" % (b, H) for b in range(4)], ["Zq"])
        for b in range(1, 4):
            mean(b, 0, H, T.Tq, "Tq", lz[:, 10:20], "landl%d" % rnd)
        scan(T.El[:], T.madd[:, 0:C], T.lv[:], 0.0, ALU.add, ALU.max, ["madd", "lv"], ["El"])
        qz(T.Zq0[:], T.Zs0[:], T.Z[:, 0:4 * H], ["Z%d0" % b for b in range(4)], ["Zq0"])
        ts(T.ll[:], T.El[:, 15:C:16], T.pc[:, 1:2], None, ALU.add, None, ["El", "pc1"], ["ll"])
        means(H, R, T.Tp, "Tp", T.zl[:, 20:34], "zl1")
        means(0, H, T.Tq, "Tq", lz[:, 0:10], "landl%d" % rnd)
        act(T.lv[:], T.Lw[:, 0:C].indirect(T.su[:]), ACT.Copy, ["Lw", "su"], ["lv"])
        for b in range(4):
            mm("P%d@v" % b, R, T.Wq[:, 128 * b:128 * b + 128], T.Ws[:, 128 * b:128 * b + 128], T.Zq[:], T.Zs[:], ["W", "Zq"])
        for b in range(4):
            mm("P%d@v" % (4 + b), H, T.Wq[:, 128 * b:128 * b + 128], T.Ws[:, 128 * b:128 * b + 128], T.Zq0[:], T.Zs0[:], ["W", "Zq0"])
        for b in range(4):
            act(T.Vp[:, C * b + H:C * b + C], T["P%d" % b][:, 0:R], ACT.Copy, ["P%d@v" % b], ["Vb%d" % b], scale=2.0 ** -5)
        for b in range(4):
            act(T.Vp[:, C * b:C * b + H], T["P%d" % (4 + b)][:, 0:H], ACT.Copy, ["P%d@v" % (4 + b)], ["Va%d" % b], scale=2.0 ** -5)
        if last:
            act(T.lf[:], T.lv[:], ACT.Copy, ["lv"], ["lf"], bias=192.0)
            dma("S", T.lb[:], T.lf[0:128:16, :], "dout", ["lf"], [])
        flush()

    for b in range(4):
        xstep(0, b)
    xstep(1, 0)
    qx(0)
    xstep(1, 1)
    xstep(1, 2)
    xstep(1, 3)
    qx(1)
    mm("P0", HF, T.vq[:], T.vs[:], T.Xq[:, 0:HF], T.Xs[:, 0:HF], ["vq", "Xq0"])
    mm("P1", HF, T.vq[:], T.vs[:], T.Xq[:, HF:C], T.Xs[:, HF:C], ["vq", "Xq1"])
    act(T.yb[:, 0:HF], T.P0[:, 0:HF], ACT.Copy, ["P0"], ["ya"])
    dma("A", T.y[:, 0:HF], T.yb[:, 0:HF], "dout", ["ya"], [])
    dma("S", T.oc[:, 0:4 * HF], T.Xq[:, 0:HF].bitcast(dt.uint8), "dout", ["Xq0"], [])
    dma("S", T.oc[:, 4 * HF:4 * C], T.Xq[:, HF:C].bitcast(dt.uint8), "dout", ["Xq1"], [])
    for k in range(4):
        dma("S" if k < 1 else "A", T.osc[4 * k:4 * k + 4, :], T.Xs[32 * k:32 * k + 4, :], "dout", ["Xq0", "Xq1"], [])
    cp(T.yb[:, HF:C], T.P1[:, 0:HF], ["P1"], ["yb"])
    dma("S", T.y[:, HF:C], T.yb[:, HF:C], "dout", ["yb"], [])
    flush()
    for s, n in total.items():
        g.sync.wait_ge(T.sem[s], n)
